import numpy as np
import ml_dtypes


def mxq(x, axis, fmt="e4m3"):
    dtype, down = {"e4m3": (ml_dtypes.float8_e4m3fn, 7), "e5m2": (ml_dtypes.float8_e5m2, 14)}[fmt]
    v = np.moveaxis(np.asarray(x, np.float32).astype(ml_dtypes.bfloat16).astype(np.float64), axis, -1)
    blocks = v.reshape(v.shape[:-1] + (-1, 32))
    amax = np.abs(blocks).max(-1, keepdims=True)
    byte = np.maximum(np.where(amax > 0, np.frexp(amax)[1] - 1 + 127, 0) - down, 1)
    scale = np.exp2(byte - 127.0)
    codes = (blocks / scale).astype(np.float32).astype(dtype).astype(np.float64)
    return np.moveaxis((codes * scale).reshape(v.shape), -1, axis)


WIDE = False


def mx_kscale(k):
    if not WIDE:
        return np.ones(k)
    levels = np.array([10, -10, 5, -5, 0])
    if k % 512:
        return np.exp2(np.random.permutation(np.resize(levels, k // 32))).repeat(32)
    a = np.empty((k // 512, 16))
    for p in range(k // 512):
        a[p, :8] = np.random.permutation(np.resize(levels, 8))
        for g in range(8):
            far = levels[np.abs(levels - a[p, g]) >= 10]
            a[p, g + 8] = far[np.random.randint(len(far))]
    return np.exp2(a.ravel()).repeat(32)


def f64(x):
    return np.asarray(x).astype(np.float64)


def striped(idx):
    return np.tile(idx.reshape(-1, 16).T, (8, 1)).astype(np.uint16)


def unstriped(offs):
    return offs[:16].T.reshape(-1).astype(np.int64)


def striped8(idx):
    return np.concatenate([x.reshape(-1, 16).T for x in idx]).astype(np.uint16)


def runs(offs, k):
    lists = np.stack([offs[16 * r : 16 * r + 16].T.reshape(-1) for r in range(8)]).astype(np.int64)
    return lists[np.arange(k) % 512 // 64]


def pack_weight(w):
    k, n = w.shape
    w = f64(np.asarray(w, np.float32).astype(ml_dtypes.bfloat16)).reshape(k // 32, 32, n)
    amax = np.abs(w).max(1)
    byte = np.clip(np.where(amax > 0, np.frexp(amax)[1] - 1 + 127 - 7, 1), 1, 254)
    scaled = (w * np.exp2(127.0 - byte)[:, None, :]).reshape(k, n).astype(np.float32)
    words = np.ascontiguousarray(scaled.reshape(k // 512, 128, 4, n).transpose(0, 1, 3, 2)).astype(ml_dtypes.float8_e4m3fn).view(np.uint8)
    return words, np.ascontiguousarray(byte.astype(np.uint8).reshape(k // 512, 16, n))


def unpack_weight(words, scales):
    g, p, n, _ = words.shape
    vals = np.ascontiguousarray(words).view(ml_dtypes.float8_e4m3fn).astype(np.float64) * np.repeat(np.exp2(scales.astype(np.float64) - 127.0), 8, axis=1)[..., None]
    return vals.transpose(0, 1, 3, 2).reshape(g * 512, n)


def sigmoid(v):
    return 1.0 / (1.0 + np.exp(-np.maximum(v, -700.0)))

def planes(y):
    n, m = y.shape
    v = y.astype(np.float32).astype(ml_dtypes.bfloat16).astype(np.float64).reshape(n // 32, 32, m)
    top = np.abs(v).max(1)
    byte = np.clip(np.where(top > 0, np.frexp(top)[1] - 1 + 127 - 7, 1), 1, 254)
    codes = (v * np.exp2(127.0 - byte)[:, None, :]).reshape(n, m).astype(np.float32).astype(ml_dtypes.float8_e4m3fn).view(np.uint8)
    words = codes.reshape(n // 512, 128, 4, m).transpose(0, 1, 3, 2)
    return np.ascontiguousarray(words), np.ascontiguousarray(byte.astype(np.uint8).reshape(n // 512, 16, m))


K, T, S, G, H, U = 512, 2048, 256, 2048, 512, 512


def setup_inputs():
    n = np.random.standard_normal
    s = mx_kscale(K)[:, None]
    packed_xT = pack_weight(n((K, T)) * s)
    packed_dT = pack_weight(n((K, G)) / s)
    perm = np.random.permutation(U)
    return {
        "x_words": packed_xT[0],
        "x_scales": packed_xT[1],
        "d_words": packed_dT[0],
        "d_scales": packed_dT[1],
        "sl": np.random.uniform(1.0, 2.0, (H, 1)).astype(np.float32),
        "th": (0.5 * n((H, 1))).astype(np.float32),
        "gs": (np.random.uniform(0.5, 1.5, (K, 1)) * s).astype(np.float32),
        "offs": striped(np.random.permutation(T)[:S]),
        "ci": striped(np.random.permutation(G)[:H]),
        "n1": striped8(np.stack([np.random.permutation(S) for _ in range(8)])),
        "n2": striped8(np.stack([np.random.permutation(S) for _ in range(8)])),
        "k1": striped8(np.random.randint(0, G, (8, H))),
        "n3": striped(perm[:S]),
        "n4": striped(perm[S:]),
        "n5": striped(np.random.permutation(U)),
    }


def reference(x_words, x_scales, d_words, d_scales, sl, th, gs, offs, ci, n1, n2, k1, n3, n4, n5):
    d_k1 = unpack_weight(d_words, d_scales)[np.arange(K)[:, None], runs(k1, K)]
    d_ci = unpack_weight(d_words, d_scales)[:, unstriped(ci)]
    xq = unpack_weight(x_words, x_scales)[:, unstriped(offs)]
    s = 0.0625 * (d_ci.T @ xq)
    st = np.maximum(s, s[np.arange(H)[:, None], runs(n1, H)])
    sg = sigmoid(f64(sl) * (st[np.arange(H)[:, None], runs(n2, H)] - f64(th)))
    z = f64(gs) * (st * sg)
    h = 0.0625 * ((d_k1.T @ mxq(z, 0, "e4m3")))
    nw = 0.5 * h
    ph = np.zeros((H, U))
    ph[:, unstriped(n3)] = h
    pg = ph.copy()
    pg[:, unstriped(n4)] = nw
    out_0 = pg - pg[:, unstriped(n5)]
    return (out_0,) + planes(out_0)

@@ -1,0 +1,195 @@
+from contextlib import ExitStack
+
+import concourse.mybir as mybir
+
+F32 = mybir.dt.float32
+BF16 = mybir.dt.bfloat16
+I32 = mybir.dt.int32
+U32 = mybir.dt.uint32
+U16 = mybir.dt.uint16
+U8 = mybir.dt.uint8
+FP8X4 = mybir.dt.float8_e4m3fn_x4
+ALU = mybir.AluOpType
+ACT = mybir.ActivationFunctionType
+
+P = 128
+PACK = 4
+K, T, S, G, H, U = 512, 2048, 256, 2048, 512, 512
+FLOPS = 2 * 2 * K * H * S
+HALF = S // 2
+PIECE = 128
+SPLIT_TILES = 2
+
+
+def tile_picked_dwqehhpagtwo_none_po_kernel(
+    tc, x_words, x_scales, d_words, d_scales, sl, th, gs, offs, ci, n1, n2, k1, n3, n4, n5, out_0, out_1, out_2
+):
+    nc = tc.nc
+    with ExitStack() as ctx:
+        keep = ctx.enter_context(tc.tile_pool(name="keep", bufs=1))
+        psum = ctx.enter_context(tc.psum_pool(name="psum", bufs=1))
+
+        def sb(shape, dtype, name, tag=None):
+            return keep.tile(shape, dtype, name=name, tag=tag or name, align_bytes=64)
+
+        def load_list(src, name):
+            tile = keep.tile(list(src.shape), U16, name=name)
+            nc.sync.dma_start(tile[:], src)
+            return tile
+
+        def entries(lst, lo, hi):
+            return lst[:, lo // 16 : hi // 16]
+
+        d_tab = sb([P, G], U32, "d_tab")
+        x_tab = sb([P, T], U32, "x_tab")
+        ds_tab = sb([P, G], U8, "ds_tab")
+        xs_tab = sb([P, T], U8, "xs_tab")
+        nc.vector.memset(ds_tab[:].bitcast(I32), 0)
+        nc.vector.memset(xs_tab[:].bitcast(I32), 0)
+
+        ci_l = load_list(ci, "ci_l")
+        offs_l = load_list(offs, "offs_l")
+        nc.sync.dma_start(d_tab[:].bitcast(I32), d_words[0].rearrange("p c r -> p (c r)").bitcast(I32))
+        nc.sync.dma_start(x_tab[:].bitcast(I32), x_words[0].rearrange("p c r -> p (c r)").bitcast(I32))
+
+        ds_rows = d_scales[0].bitcast(I32)
+        xs_rows = x_scales[0].bitcast(I32)
+        for r in range(2):
+            nc.scalar.dma_start(ds_tab[:].bitcast(I32)[r:P:16, :], ds_rows[r:16:2, :])
+        for r in range(2, 4):
+            nc.scalar.dma_start(ds_tab[:].bitcast(I32)[r:P:32, :], ds_rows[r:16:4, :])
+        for q in range(4):
+            nc.scalar.dma_start(xs_tab[:].bitcast(I32)[32 * q : 32 * q + 4, :], xs_rows[4 * q : 4 * q + 4, :])
+
+        n1_l = load_list(n1, "n1_l")
+        k1_l = load_list(k1, "k1_l")
+
+        sl_t = sb([P, PACK], F32, "sl_t")
+        th_t = sb([P, PACK], F32, "th_t")
+        gs_t = sb([P, PACK], F32, "gs_t")
+        for tile, src in ((sl_t, sl), (th_t, th), (gs_t, gs)):
+            nc.sync.dma_start(tile[:], src.rearrange("(p t) o -> p (t o)", t=PACK))
+        n2_l = load_list(n2, "n2_l")
+        n3_l = load_list(n3, "n3_l")
+        n4_l = load_list(n4, "n4_l")
+        n5_l = load_list(n5, "n5_l")
+        wk_s = sb([P, H], U8, "wk_s")
+        nc.vector.memset(wk_s[:].bitcast(I32), 0)
+
+        wc_s = sb([P, H], U8, "wc_s")
+        wc_w = sb([P, H], U32, "wc_w")
+        xq_s = sb([P, S], U8, "xq_s")
+        xq_w = sb([P, S], U32, "xq_w")
+        nc.vector.tensor_copy(wc_s[:].rearrange("p (t m) -> p m t", t=PACK), ds_tab[:].indirect(ci_l[:]))
+        nc.vector.tensor_copy(wc_w[:].rearrange("p (t m) -> p m t", t=PACK), d_tab[:].indirect(ci_l[:]))
+        nc.vector.tensor_copy(xq_s[:], xs_tab[:].indirect(offs_l[:]))
+        nc.vector.tensor_copy(xq_w[:], x_tab[:].indirect(offs_l[:]))
+
+        s_ps = [psum.tile([P, S], F32, name=f"s_ps{t}") for t in range(PACK)]
+        for t in range(PACK):
+            cols = slice(P * t, P * (t + 1))
+            nc.tensor.matmul_mx(
+                out=s_ps[t][:], lhsT=wc_w[:, cols].bitcast(FP8X4), lhsT_scale=wc_s[:, cols],
+                rhs=xq_w[:].bitcast(FP8X4), rhs_scale=xq_s[:], start=True, stop=True,
+            )
+
+        gk_s = sb([P, H], U8, "gk_s", tag="x_tab")
+        gk_w = sb([P, H], U32, "gk_w", tag="wc_w")
+        dk_s = sb([P, H], U8, "dk_s")
+        wk_w = sb([P, H], U32, "wk_w")
+        nc.vector.tensor_copy(gk_s[:], ds_tab[:].indirect(k1_l[:]))
+        nc.vector.tensor_copy(dk_s[:].rearrange("p (t m) -> p m t", t=PACK), gk_s[:].rearrange("p (m t) -> p m t", t=PACK))
+        for r, src in enumerate((0, 1, 16, 17)):
+            nc.sync.dma_start(wk_s[:].bitcast(I32)[r:P:32, :], dk_s[:].bitcast(I32)[src:P:32, :])
+
+        bias_t = sb([P, PACK], F32, "bias_t")
+        nc.vector.scalar_tensor_tensor(bias_t[:], sl_t[:], -1.0, th_t[:], ALU.mult, ALU.mult)
+
+        s_win = [sb([P, 2 * S], F32, f"s_win{t}") for t in range(PACK)]
+        s_n1 = sb([P, PACK, S], F32, "s_n1")
+        st = [sb([P, S], F32, f"st{t}") for t in range(PACK)]
+        for t in range(PACK):
+            nc.scalar.activation(s_win[t][:, :S], s_ps[t][:], ACT.Copy, scale=0.0625)
+        for t in range(PACK):
+            nc.scalar.activation(s_n1[:, t, :], s_win[t][:].indirect(n1_l[:]), ACT.Copy)
+            nc.vector.tensor_tensor(st[t][:], s_win[t][:, :S], s_n1[:, t, :], ALU.max)
+
+        nc.vector.tensor_copy(gk_w[:], d_tab[:].indirect(k1_l[:]))
+        nc.vector.tensor_copy(
+            wk_w[:].rearrange("p (t c i) -> p c t i", t=PACK, i=4),
+            gk_w[:].rearrange("p (c i t) -> p c t i", t=PACK, i=4),
+        )
+
+        sg = sb([P, PACK, S], F32, "sg")
+        z_b = sb([P, PACK, S], BF16, "z_b")
+        z_i = sb([P, S, PACK], BF16, "z_i")
+        z_w = sb([P, S], U32, "z_w")
+        z_s = sb([P, S], U8, "z_s")
+        h_ps = [psum.tile([P, S], F32, name=f"h_ps{t}") for t in range(PACK)]
+        h_sb = sb([P, PACK, S], F32, "h_sb")
+        pg = [sb([P, U], F32, f"pg{t}") for t in range(PACK)]
+
+        def scatter(tiles, lo, hi):
+            for lst, factor in ((n3_l, 1.0), (n4_l, 0.5)):
+                for t in tiles:
+                    nc.scalar.activation(pg[t][:].indirect(entries(lst, lo, hi)), h_sb[:, t, lo:hi], ACT.Copy, scale=factor)
+
+        halves = [(lo, lo + HALF) for lo in range(0, S, HALF)]
+        for lo, hi in halves:
+            for t in range(PACK):
+                nc.scalar.activation(
+                    sg[:, t, lo:hi], st[t][:].indirect(entries(n2_l, lo, hi)), ACT.Sigmoid,
+                    scale=sl_t[:, t : t + 1], bias=bias_t[:, t : t + 1],
+                )
+        for lo, hi in halves:
+            for t in range(PACK):
+                nc.vector.scalar_tensor_tensor(
+                    z_b[:, t, lo:hi], st[t][:, lo:hi], gs_t[:, t : t + 1], sg[:, t, lo:hi], ALU.mult, ALU.mult
+                )
+            nc.vector.tensor_copy(
+                z_i[:, lo:hi, :].rearrange("p (c i) t -> p c t i", i=4),
+                z_b[:, :, lo:hi].rearrange("p t (c i) -> p c t i", i=4),
+            )
+            nc.vector.quantize_mx(
+                out=z_w[:, lo:hi].bitcast(FP8X4), scales=z_s[:, lo:hi],
+                in_=z_i[:, lo:hi, :].rearrange("p c t -> p (c t)"),
+            )
+            for t in range(PACK):
+                cols = slice(P * t, P * (t + 1))
+                nc.tensor.matmul_mx(
+                    out=h_ps[t][:, lo:hi], lhsT=wk_w[:, cols].bitcast(FP8X4), lhsT_scale=wk_s[:, cols],
+                    rhs=z_w[:, lo:hi].bitcast(FP8X4), rhs_scale=z_s[:, lo:hi], start=True, stop=True,
+                )
+            for t in range(SPLIT_TILES):
+                nc.vector.tensor_scalar(h_sb[:, t, lo:hi], h_ps[t][:, lo:hi], 0.0625, None, ALU.mult)
+            scatter(range(SPLIT_TILES), lo, hi)
+        for t in range(SPLIT_TILES, PACK):
+            nc.vector.tensor_scalar(h_sb[:, t, :], h_ps[t][:], 0.0625, None, ALU.mult)
+        scatter(range(SPLIT_TILES, PACK), 0, S)
+
+        pg_n5 = sb([P, PACK, U], F32, "pg_n5")
+        y = sb([P, PACK, U], F32, "y")
+        y_i = sb([P, U, PACK], BF16, "y_i")
+        y_w = sb([P, U], U32, "y_w")
+        y_s = sb([P, U], U8, "y_s")
+        out_rows = out_0.rearrange("(p t) w -> p t w", t=PACK)
+        out_words = out_1[0].rearrange("p c r -> p (c r)").bitcast(I32)
+        for lo in range(0, U, PIECE):
+            hi = lo + PIECE
+            for t in range(PACK):
+                nc.scalar.activation(pg_n5[:, t, lo:hi], pg[t][:].indirect(entries(n5_l, lo, hi)), ACT.Copy)
+                nc.vector.tensor_tensor(y[:, t, lo:hi], pg[t][:, lo:hi], pg_n5[:, t, lo:hi], ALU.subtract)
+            nc.sync.dma_start(out_rows[:, :, lo:hi], y[:, :, lo:hi])
+            nc.vector.tensor_copy(
+                y_i[:, lo:hi, :].rearrange("p (c i) t -> p c t i", i=4),
+                y[:, :, lo:hi].rearrange("p t (c i) -> p c t i", i=4),
+            )
+            nc.vector.quantize_mx(
+                out=y_w[:, lo:hi].bitcast(FP8X4), scales=y_s[:, lo:hi],
+                in_=y_i[:, lo:hi, :].rearrange("p c t -> p (c t)"),
+            )
+            nc.sync.dma_start(out_words[:, lo:hi], y_w[:, lo:hi].bitcast(I32))
+        scale_rows = out_2[0].bitcast(I32)
+        for q in range(4):
+            eng = nc.sync if q % 2 else nc.scalar
+            eng.dma_start(scale_rows[4 * q : 4 * q + 4, :], y_s[:].bitcast(I32)[32 * q : 32 * q + 4, :])

@@ -61,6 +61,9 @@ def tile_picked_dwqehhpagtwo_none_po_kernel(
         for q in range(4):
             nc.scalar.dma_start(xs_tab[:].bitcast(I32)[32 * q : 32 * q + 4, :], xs_rows[4 * q : 4 * q + 4, :])
 
+        warm = sb([P, 2], F32, "warm")
+        nc.vector.memset(warm[:, 0:1], 0.0)
+        nc.scalar.activation(warm[:, 1:2], warm[:, 0:1], ACT.Sigmoid)
         n1_l = load_list(n1, "n1_l")
         k1_l = load_list(k1, "k1_l")
 

@@ -19,6 +19,10 @@ FLOPS = 2 * 2 * K * H * S
 HALF = S // 2
 PIECE = 128
 SPLIT_TILES = 2
+D_FIRST = 512
+X_ROW = 4
+S_ON_SCALAR = 3
+X_FIRST = 1024
 
 
 def tile_picked_dwqehhpagtwo_none_po_kernel(
@@ -40,6 +44,15 @@ def tile_picked_dwqehhpagtwo_none_po_kernel(
         def entries(lst, lo, hi):
             return lst[:, lo // 16 : hi // 16]
 
+        def deal_bytes(dst, src):
+            nc.vector.tensor_copy(dst[:].rearrange("p (t m) -> p t m", t=PACK), src[:].rearrange("p (m t) -> p t m", t=PACK))
+
+        def deal_words(dst, src):
+            nc.vector.tensor_copy(
+                dst[:].rearrange("p (t c i) -> p c t i", t=PACK, i=4),
+                src[:].rearrange("p (c i t) -> p c t i", t=PACK, i=4),
+            )
+
         d_tab = sb([P, G], U32, "d_tab")
         x_tab = sb([P, T], U32, "x_tab")
         ds_tab = sb([P, G], U8, "ds_tab")
@@ -47,25 +60,28 @@ def tile_picked_dwqehhpagtwo_none_po_kernel(
         nc.vector.memset(ds_tab[:].bitcast(I32), 0)
         nc.vector.memset(xs_tab[:].bitcast(I32), 0)
 
-        ci_l = load_list(ci, "ci_l")
-        offs_l = load_list(offs, "offs_l")
-        nc.sync.dma_start(d_tab[:].bitcast(I32), d_words[0].rearrange("p c r -> p (c r)").bitcast(I32))
-        nc.sync.dma_start(x_tab[:].bitcast(I32), x_words[0].rearrange("p c r -> p (c r)").bitcast(I32))
-
+        d_src = d_words[0].rearrange("p c r -> p (c r)").bitcast(I32)
         ds_rows = d_scales[0].bitcast(I32)
         xs_rows = x_scales[0].bitcast(I32)
+        x_src = x_words[0].rearrange("p c r -> p (c r)").bitcast(I32)
+        nc.sync.dma_start(d_tab[:].bitcast(I32)[:, :D_FIRST], d_src[:, :D_FIRST])
+        ci_l = load_list(ci, "ci_l")
         for r in range(2):
-            nc.scalar.dma_start(ds_tab[:].bitcast(I32)[r:P:16, :], ds_rows[r:16:2, :])
+            nc.sync.dma_start(ds_tab[:].bitcast(I32)[r:P:16, :], ds_rows[r:16:2, :])
         for r in range(2, 4):
-            nc.scalar.dma_start(ds_tab[:].bitcast(I32)[r:P:32, :], ds_rows[r:16:4, :])
+            nc.sync.dma_start(ds_tab[:].bitcast(I32)[r:P:32, :], ds_rows[r:16:4, :])
+        nc.sync.dma_start(d_tab[:].bitcast(I32)[:, D_FIRST:], d_src[:, D_FIRST:])
+        nc.sync.dma_start(x_tab[:].bitcast(I32)[:, :X_FIRST], x_src[:, :X_FIRST])
+        offs_l = load_list(offs, "offs_l")
         for q in range(4):
-            nc.scalar.dma_start(xs_tab[:].bitcast(I32)[32 * q : 32 * q + 4, :], xs_rows[4 * q : 4 * q + 4, :])
+            nc.sync.dma_start(xs_tab[:].bitcast(I32)[32 * q + X_ROW : 32 * q + X_ROW + 4, :], xs_rows[4 * q : 4 * q + 4, :])
+        nc.sync.dma_start(x_tab[:].bitcast(I32)[:, X_FIRST:], x_src[:, X_FIRST:])
 
         warm = sb([P, 2], F32, "warm")
         nc.vector.memset(warm[:, 0:1], 0.0)
         nc.scalar.activation(warm[:, 1:2], warm[:, 0:1], ACT.Sigmoid)
-        n1_l = load_list(n1, "n1_l")
         k1_l = load_list(k1, "k1_l")
+        n1_l = load_list(n1, "n1_l")
 
         sl_t = sb([P, PACK], F32, "sl_t")
         th_t = sb([P, PACK], F32, "th_t")
@@ -83,9 +99,13 @@ def tile_picked_dwqehhpagtwo_none_po_kernel(
         wc_w = sb([P, H], U32, "wc_w")
         xq_s = sb([P, S], U8, "xq_s")
         xq_w = sb([P, S], U32, "xq_w")
-        nc.vector.tensor_copy(wc_s[:].rearrange("p (t m) -> p m t", t=PACK), ds_tab[:].indirect(ci_l[:]))
-        nc.vector.tensor_copy(wc_w[:].rearrange("p (t m) -> p m t", t=PACK), d_tab[:].indirect(ci_l[:]))
+        gc_s = sb([P, H], U8, "gc_s")
+        gc_w = sb([P, H], U32, "gc_w")
+        nc.vector.tensor_copy(gc_s[:], ds_tab[:].indirect(ci_l[:]))
+        deal_bytes(wc_s, gc_s)
+        nc.vector.tensor_copy(gc_w[:], d_tab[:].indirect(ci_l[:]))
         nc.vector.tensor_copy(xq_s[:], xs_tab[:].indirect(offs_l[:]))
+        deal_words(wc_w, gc_w)
         nc.vector.tensor_copy(xq_w[:], x_tab[:].indirect(offs_l[:]))
 
         s_ps = [psum.tile([P, S], F32, name=f"s_ps{t}") for t in range(PACK)]
@@ -93,7 +113,7 @@ def tile_picked_dwqehhpagtwo_none_po_kernel(
             cols = slice(P * t, P * (t + 1))
             nc.tensor.matmul_mx(
                 out=s_ps[t][:], lhsT=wc_w[:, cols].bitcast(FP8X4), lhsT_scale=wc_s[:, cols],
-                rhs=xq_w[:].bitcast(FP8X4), rhs_scale=xq_s[:], start=True, stop=True,
+                rhs=xq_w[:].bitcast(FP8X4), rhs_scale=xq_s[X_ROW:P, :], start=True, stop=True,
             )
 
         gk_s = sb([P, H], U8, "gk_s", tag="x_tab")
@@ -101,30 +121,31 @@ def tile_picked_dwqehhpagtwo_none_po_kernel(
         dk_s = sb([P, H], U8, "dk_s")
         wk_w = sb([P, H], U32, "wk_w")
         nc.vector.tensor_copy(gk_s[:], ds_tab[:].indirect(k1_l[:]))
-        nc.vector.tensor_copy(dk_s[:].rearrange("p (t m) -> p m t", t=PACK), gk_s[:].rearrange("p (m t) -> p m t", t=PACK))
+        deal_bytes(dk_s, gk_s)
         for r, src in enumerate((0, 1, 16, 17)):
             nc.sync.dma_start(wk_s[:].bitcast(I32)[r:P:32, :], dk_s[:].bitcast(I32)[src:P:32, :])
 
         bias_t = sb([P, PACK], F32, "bias_t")
-        nc.vector.scalar_tensor_tensor(bias_t[:], sl_t[:], -1.0, th_t[:], ALU.mult, ALU.mult)
+        slth = sb([P, PACK], F32, "slth")
+        nc.gpsimd.tensor_tensor(slth[:], sl_t[:], th_t[:], ALU.mult)
+        nc.gpsimd.tensor_scalar(bias_t[:], slth[:], -1.0, 0.0, ALU.mult, ALU.add)
 
         s_win = [sb([P, 2 * S], F32, f"s_win{t}") for t in range(PACK)]
         s_n1 = sb([P, PACK, S], F32, "s_n1")
         st = [sb([P, S], F32, f"st{t}") for t in range(PACK)]
         for t in range(PACK):
-            nc.scalar.activation(s_win[t][:, :S], s_ps[t][:], ACT.Copy, scale=0.0625)
+            if t < S_ON_SCALAR:
+                nc.scalar.activation(s_win[t][:, :S], s_ps[t][:], ACT.Copy, scale=0.0625)
+            else:
+                nc.vector.tensor_scalar(s_win[t][:, :S], s_ps[t][:], 0.0625, None, ALU.mult)
+        nc.vector.tensor_copy(gk_w[:], d_tab[:].indirect(k1_l[:]))
         for t in range(PACK):
             nc.scalar.activation(s_n1[:, t, :], s_win[t][:].indirect(n1_l[:]), ACT.Copy)
             nc.vector.tensor_tensor(st[t][:], s_win[t][:, :S], s_n1[:, t, :], ALU.max)
 
-        nc.vector.tensor_copy(gk_w[:], d_tab[:].indirect(k1_l[:]))
-        nc.vector.tensor_copy(
-            wk_w[:].rearrange("p (t c i) -> p c t i", t=PACK, i=4),
-            gk_w[:].rearrange("p (c i t) -> p c t i", t=PACK, i=4),
-        )
 
-        sg = sb([P, PACK, S], F32, "sg")
-        z_b = sb([P, PACK, S], BF16, "z_b")
+        deal_words(wk_w, gk_w)
+        sg = [sb([P, PACK, HALF], F32, "sg0"), sb([P, PACK, HALF], F32, "sg1", tag="s_n1")]
         z_i = sb([P, S, PACK], BF16, "z_i")
         z_w = sb([P, S], U32, "z_w")
         z_s = sb([P, S], U8, "z_s")
@@ -138,20 +159,21 @@ def tile_picked_dwqehhpagtwo_none_po_kernel(
                     nc.scalar.activation(pg[t][:].indirect(entries(lst, lo, hi)), h_sb[:, t, lo:hi], ACT.Copy, scale=factor)
 
         halves = [(lo, lo + HALF) for lo in range(0, S, HALF)]
-        for lo, hi in halves:
+        for c, (lo, hi) in enumerate(halves):
             for t in range(PACK):
                 nc.scalar.activation(
-                    sg[:, t, lo:hi], st[t][:].indirect(entries(n2_l, lo, hi)), ACT.Sigmoid,
+                    sg[c][:, t, :], st[t][:].indirect(entries(n2_l, lo, hi)), ACT.Sigmoid,
                     scale=sl_t[:, t : t + 1], bias=bias_t[:, t : t + 1],
                 )
-        for lo, hi in halves:
+        for c, (lo, hi) in enumerate(halves):
+            z_b = sb([P, PACK, HALF], BF16, f"z_b{c}", tag="z_b")
             for t in range(PACK):
                 nc.vector.scalar_tensor_tensor(
-                    z_b[:, t, lo:hi], st[t][:, lo:hi], gs_t[:, t : t + 1], sg[:, t, lo:hi], ALU.mult, ALU.mult
+                    z_b[:, t, :], st[t][:, lo:hi], gs_t[:, t : t + 1], sg[c][:, t, :], ALU.mult, ALU.mult
                 )
             nc.vector.tensor_copy(
                 z_i[:, lo:hi, :].rearrange("p (c i) t -> p c t i", i=4),
-                z_b[:, :, lo:hi].rearrange("p t (c i) -> p c t i", i=4),
+                z_b[:].rearrange("p t (c i) -> p c t i", i=4),
             )
             nc.vector.quantize_mx(
                 out=z_w[:, lo:hi].bitcast(FP8X4), scales=z_s[:, lo:hi],
@@ -164,7 +186,10 @@ def tile_picked_dwqehhpagtwo_none_po_kernel(
                     rhs=z_w[:, lo:hi].bitcast(FP8X4), rhs_scale=z_s[:, lo:hi], start=True, stop=True,
                 )
             for t in range(SPLIT_TILES):
-                nc.vector.tensor_scalar(h_sb[:, t, lo:hi], h_ps[t][:, lo:hi], 0.0625, None, ALU.mult)
+                if lo == 0:
+                    nc.scalar.activation(h_sb[:, t, lo:hi], h_ps[t][:, lo:hi], ACT.Copy, scale=0.0625)
+                else:
+                    nc.vector.tensor_scalar(h_sb[:, t, lo:hi], h_ps[t][:, lo:hi], 0.0625, None, ALU.mult)
             scatter(range(SPLIT_TILES), lo, hi)
         for t in range(SPLIT_TILES, PACK):
             nc.vector.tensor_scalar(h_sb[:, t, :], h_ps[t][:], 0.0625, None, ALU.mult)

@@ -19,6 +19,7 @@ FLOPS = 2 * 2 * K * H * S
 HALF = S // 2
 PIECE = 128
 SPLIT_TILES = 2
+EARLY_TILES = 2
 D_FIRST = 512
 X_ROW = 4
 S_ON_SCALAR = 3
@@ -151,12 +152,11 @@ def tile_picked_dwqehhpagtwo_none_po_kernel(
         z_s = sb([P, S], U8, "z_s")
         h_ps = [psum.tile([P, S], F32, name=f"h_ps{t}") for t in range(PACK)]
         h_sb = sb([P, PACK, S], F32, "h_sb")
-        pg = [sb([P, U], F32, f"pg{t}") for t in range(PACK)]
+        pg = [sb([P, 2 * U if t < EARLY_TILES else U], F32, f"pg{t}") for t in range(PACK)]
 
-        def scatter(tiles, lo, hi):
-            for lst, factor in ((n3_l, 1.0), (n4_l, 0.5)):
-                for t in tiles:
-                    nc.scalar.activation(pg[t][:].indirect(entries(lst, lo, hi)), h_sb[:, t, lo:hi], ACT.Copy, scale=factor)
+        def scatter(lst, factor, tiles, lo, hi):
+            for t in tiles:
+                nc.scalar.activation(pg[t][:].indirect(entries(lst, lo, hi)), h_sb[:, t, lo:hi], ACT.Copy, scale=factor)
 
         halves = [(lo, lo + HALF) for lo in range(0, S, HALF)]
         for c, (lo, hi) in enumerate(halves):
@@ -190,10 +190,9 @@ def tile_picked_dwqehhpagtwo_none_po_kernel(
                     nc.scalar.activation(h_sb[:, t, lo:hi], h_ps[t][:, lo:hi], ACT.Copy, scale=0.0625)
                 else:
                     nc.vector.tensor_scalar(h_sb[:, t, lo:hi], h_ps[t][:, lo:hi], 0.0625, None, ALU.mult)
-            scatter(range(SPLIT_TILES), lo, hi)
+            scatter(n3_l, 1.0, range(SPLIT_TILES), lo, hi)
         for t in range(SPLIT_TILES, PACK):
             nc.vector.tensor_scalar(h_sb[:, t, :], h_ps[t][:], 0.0625, None, ALU.mult)
-        scatter(range(SPLIT_TILES, PACK), 0, S)
 
         pg_n5 = sb([P, PACK, U], F32, "pg_n5")
         y = sb([P, PACK, U], F32, "y")
@@ -202,21 +201,40 @@ def tile_picked_dwqehhpagtwo_none_po_kernel(
         y_s = sb([P, U], U8, "y_s")
         out_rows = out_0.rearrange("(p t) w -> p t w", t=PACK)
         out_words = out_1[0].rearrange("p c r -> p (c r)").bitcast(I32)
-        for lo in range(0, U, PIECE):
-            hi = lo + PIECE
-            for t in range(PACK):
+
+        def subtract(tiles, lo, hi):
+            for t in tiles:
                 nc.scalar.activation(pg_n5[:, t, lo:hi], pg[t][:].indirect(entries(n5_l, lo, hi)), ACT.Copy)
                 nc.vector.tensor_tensor(y[:, t, lo:hi], pg[t][:, lo:hi], pg_n5[:, t, lo:hi], ALU.subtract)
-            nc.sync.dma_start(out_rows[:, :, lo:hi], y[:, :, lo:hi])
+
+        def store(tiles, lo, hi):
+            nc.sync.dma_start(out_rows[:, tiles.start : tiles.stop, lo:hi], y[:, tiles.start : tiles.stop, lo:hi])
+
+        def round_pair(tiles, lo, hi):
             nc.vector.tensor_copy(
-                y_i[:, lo:hi, :].rearrange("p (c i) t -> p c t i", i=4),
-                y[:, :, lo:hi].rearrange("p t (c i) -> p c t i", i=4),
+                y_i[:, lo:hi, tiles.start : tiles.stop].rearrange("p (c i) t -> p c t i", i=4),
+                y[:, tiles.start : tiles.stop, lo:hi].rearrange("p t (c i) -> p c t i", i=4),
             )
+
+        early, late = range(EARLY_TILES), range(EARLY_TILES, PACK)
+        scatter(n4_l, 0.5, early, 0, S)
+        scatter(n3_l, 1.0, late, 0, S)
+        subtract(early, 0, U)
+        store(early, 0, U)
+        round_pair(early, 0, U)
+        scatter(n4_l, 0.5, late, 0, S)
+        for lo in range(0, U, PIECE):
+            hi = lo + PIECE
+            subtract(late, lo, hi)
+            if hi % (2 * PIECE) == 0:
+                store(late, hi - 2 * PIECE, hi)
+            round_pair(late, lo, hi)
             nc.vector.quantize_mx(
                 out=y_w[:, lo:hi].bitcast(FP8X4), scales=y_s[:, lo:hi],
                 in_=y_i[:, lo:hi, :].rearrange("p c t -> p (c t)"),
             )
-            nc.sync.dma_start(out_words[:, lo:hi], y_w[:, lo:hi].bitcast(I32))
+            if hi % (2 * PIECE) == 0:
+                nc.sync.dma_start(out_words[:, hi - 2 * PIECE : hi], y_w[:, hi - 2 * PIECE : hi].bitcast(I32))
         scale_rows = out_2[0].bitcast(I32)
         for q in range(4):
             eng = nc.sync if q % 2 else nc.scalar

from contextlib import ExitStack

import concourse.mybir as mybir

F32 = mybir.dt.float32
BF16 = mybir.dt.bfloat16
I32 = mybir.dt.int32
U32 = mybir.dt.uint32
U16 = mybir.dt.uint16
U8 = mybir.dt.uint8
FP8X4 = mybir.dt.float8_e4m3fn_x4
ALU = mybir.AluOpType
ACT = mybir.ActivationFunctionType

P = 128
PACK = 4
K, T, S, G, H, U = 512, 2048, 256, 2048, 512, 512
FLOPS = 2 * 2 * K * H * S
HALF = S // 2
PIECE = 128
SPLIT_TILES = 2
EARLY_TILES = 2
D_FIRST = 512
X_ROW = 4
S_ON_SCALAR = 3
X_FIRST = 1024


def tile_picked_dwqehhpagtwo_none_po_kernel(
    tc, x_words, x_scales, d_words, d_scales, sl, th, gs, offs, ci, n1, n2, k1, n3, n4, n5, out_0, out_1, out_2
):
    nc = tc.nc
    with ExitStack() as ctx:
        keep = ctx.enter_context(tc.tile_pool(name="keep", bufs=1))
        psum = ctx.enter_context(tc.psum_pool(name="psum", bufs=1))

        def sb(shape, dtype, name, tag=None):
            return keep.tile(shape, dtype, name=name, tag=tag or name, align_bytes=64)

        def load_list(src, name):
            tile = keep.tile(list(src.shape), U16, name=name)
            nc.sync.dma_start(tile[:], src)
            return tile

        def entries(lst, lo, hi):
            return lst[:, lo // 16 : hi // 16]

        def deal_bytes(dst, src):
            nc.vector.tensor_copy(dst[:].rearrange("p (t m) -> p t m", t=PACK), src[:].rearrange("p (m t) -> p t m", t=PACK))

        def deal_words(dst, src):
            nc.vector.tensor_copy(
                dst[:].rearrange("p (t c i) -> p c t i", t=PACK, i=4),
                src[:].rearrange("p (c i t) -> p c t i", t=PACK, i=4),
            )

        d_tab = sb([P, G], U32, "d_tab")
        x_tab = sb([P, T], U32, "x_tab")
        ds_tab = sb([P, G], U8, "ds_tab")
        xs_tab = sb([P, T], U8, "xs_tab")
        nc.vector.memset(ds_tab[:].bitcast(I32), 0)
        nc.vector.memset(xs_tab[:].bitcast(I32), 0)

        d_src = d_words[0].rearrange("p c r -> p (c r)").bitcast(I32)
        ds_rows = d_scales[0].bitcast(I32)
        xs_rows = x_scales[0].bitcast(I32)
        x_src = x_words[0].rearrange("p c r -> p (c r)").bitcast(I32)
        nc.sync.dma_start(d_tab[:].bitcast(I32)[:, :D_FIRST], d_src[:, :D_FIRST])
        ci_l = load_list(ci, "ci_l")
        for r in range(2):
            nc.sync.dma_start(ds_tab[:].bitcast(I32)[r:P:16, :], ds_rows[r:16:2, :])
        for r in range(2, 4):
            nc.sync.dma_start(ds_tab[:].bitcast(I32)[r:P:32, :], ds_rows[r:16:4, :])
        nc.sync.dma_start(d_tab[:].bitcast(I32)[:, D_FIRST:], d_src[:, D_FIRST:])
        nc.sync.dma_start(x_tab[:].bitcast(I32)[:, :X_FIRST], x_src[:, :X_FIRST])
        offs_l = load_list(offs, "offs_l")
        for q in range(4):
            nc.sync.dma_start(xs_tab[:].bitcast(I32)[32 * q + X_ROW : 32 * q + X_ROW + 4, :], xs_rows[4 * q : 4 * q + 4, :])
        nc.sync.dma_start(x_tab[:].bitcast(I32)[:, X_FIRST:], x_src[:, X_FIRST:])

        warm = sb([P, 2], F32, "warm")
        nc.vector.memset(warm[:, 0:1], 0.0)
        nc.scalar.activation(warm[:, 1:2], warm[:, 0:1], ACT.Sigmoid)
        k1_l = load_list(k1, "k1_l")
        n1_l = load_list(n1, "n1_l")

        sl_t = sb([P, PACK], F32, "sl_t")
        th_t = sb([P, PACK], F32, "th_t")
        gs_t = sb([P, PACK], F32, "gs_t")
        for tile, src in ((sl_t, sl), (th_t, th), (gs_t, gs)):
            nc.sync.dma_start(tile[:], src.rearrange("(p t) o -> p (t o)", t=PACK))
        n2_l = load_list(n2, "n2_l")
        n3_l = load_list(n3, "n3_l")
        n4_l = load_list(n4, "n4_l")
        n5_l = load_list(n5, "n5_l")
        wk_s = sb([P, H], U8, "wk_s")
        nc.vector.memset(wk_s[:].bitcast(I32), 0)

        wc_s = sb([P, H], U8, "wc_s")
        wc_w = sb([P, H], U32, "wc_w")
        xq_s = sb([P, S], U8, "xq_s")
        xq_w = sb([P, S], U32, "xq_w")
        gc_s = sb([P, H], U8, "gc_s")
        gc_w = sb([P, H], U32, "gc_w")
        nc.vector.tensor_copy(gc_s[:], ds_tab[:].indirect(ci_l[:]))
        deal_bytes(wc_s, gc_s)
        nc.vector.tensor_copy(gc_w[:], d_tab[:].indirect(ci_l[:]))
        nc.vector.tensor_copy(xq_s[:], xs_tab[:].indirect(offs_l[:]))
        deal_words(wc_w, gc_w)
        nc.vector.tensor_copy(xq_w[:], x_tab[:].indirect(offs_l[:]))

        s_ps = [psum.tile([P, S], F32, name=f"s_ps{t}") for t in range(PACK)]
        for t in range(PACK):
            cols = slice(P * t, P * (t + 1))
            nc.tensor.matmul_mx(
                out=s_ps[t][:], lhsT=wc_w[:, cols].bitcast(FP8X4), lhsT_scale=wc_s[:, cols],
                rhs=xq_w[:].bitcast(FP8X4), rhs_scale=xq_s[X_ROW:P, :], start=True, stop=True,
            )

        gk_s = sb([P, H], U8, "gk_s", tag="x_tab")
        gk_w = sb([P, H], U32, "gk_w", tag="wc_w")
        dk_s = sb([P, H], U8, "dk_s")
        wk_w = sb([P, H], U32, "wk_w")
        nc.vector.tensor_copy(gk_s[:], ds_tab[:].indirect(k1_l[:]))
        deal_bytes(dk_s, gk_s)
        for r, src in enumerate((0, 1, 16, 17)):
            nc.sync.dma_start(wk_s[:].bitcast(I32)[r:P:32, :], dk_s[:].bitcast(I32)[src:P:32, :])

        bias_t = sb([P, PACK], F32, "bias_t")
        slth = sb([P, PACK], F32, "slth")
        nc.gpsimd.tensor_tensor(slth[:], sl_t[:], th_t[:], ALU.mult)
        nc.gpsimd.tensor_scalar(bias_t[:], slth[:], -1.0, 0.0, ALU.mult, ALU.add)

        s_win = [sb([P, 2 * S], F32, f"s_win{t}") for t in range(PACK)]
        s_n1 = sb([P, PACK, S], F32, "s_n1")
        st = [sb([P, S], F32, f"st{t}") for t in range(PACK)]
        for t in range(PACK):
            if t < S_ON_SCALAR:
                nc.scalar.activation(s_win[t][:, :S], s_ps[t][:], ACT.Copy, scale=0.0625)
            else:
                nc.vector.tensor_scalar(s_win[t][:, :S], s_ps[t][:], 0.0625, None, ALU.mult)
        nc.vector.tensor_copy(gk_w[:], d_tab[:].indirect(k1_l[:]))
        for t in range(PACK):
            nc.scalar.activation(s_n1[:, t, :], s_win[t][:].indirect(n1_l[:]), ACT.Copy)
            nc.vector.tensor_tensor(st[t][:], s_win[t][:, :S], s_n1[:, t, :], ALU.max)


        deal_words(wk_w, gk_w)
        sg = [sb([P, PACK, HALF], F32, "sg0"), sb([P, PACK, HALF], F32, "sg1", tag="s_n1")]
        z_i = sb([P, S, PACK], BF16, "z_i")
        z_w = sb([P, S], U32, "z_w")
        z_s = sb([P, S], U8, "z_s")
        h_ps = [psum.tile([P, S], F32, name=f"h_ps{t}") for t in range(PACK)]
        h_sb = sb([P, PACK, S], F32, "h_sb")
        pg = [sb([P, 2 * U if t < EARLY_TILES else U], F32, f"pg{t}") for t in range(PACK)]

        def scatter(lst, factor, tiles, lo, hi):
            for t in tiles:
                nc.scalar.activation(pg[t][:].indirect(entries(lst, lo, hi)), h_sb[:, t, lo:hi], ACT.Copy, scale=factor)

        halves = [(lo, lo + HALF) for lo in range(0, S, HALF)]
        for c, (lo, hi) in enumerate(halves):
            for t in range(PACK):
                nc.scalar.activation(
                    sg[c][:, t, :], st[t][:].indirect(entries(n2_l, lo, hi)), ACT.Sigmoid,
                    scale=sl_t[:, t : t + 1], bias=bias_t[:, t : t + 1],
                )
        for c, (lo, hi) in enumerate(halves):
            z_b = sb([P, PACK, HALF], BF16, f"z_b{c}", tag="z_b")
            for t in range(PACK):
                nc.vector.scalar_tensor_tensor(
                    z_b[:, t, :], st[t][:, lo:hi], gs_t[:, t : t + 1], sg[c][:, t, :], ALU.mult, ALU.mult
                )
            nc.vector.tensor_copy(
                z_i[:, lo:hi, :].rearrange("p (c i) t -> p c t i", i=4),
                z_b[:].rearrange("p t (c i) -> p c t i", i=4),
            )
            nc.vector.quantize_mx(
                out=z_w[:, lo:hi].bitcast(FP8X4), scales=z_s[:, lo:hi],
                in_=z_i[:, lo:hi, :].rearrange("p c t -> p (c t)"),
            )
            for t in range(PACK):
                cols = slice(P * t, P * (t + 1))
                nc.tensor.matmul_mx(
                    out=h_ps[t][:, lo:hi], lhsT=wk_w[:, cols].bitcast(FP8X4), lhsT_scale=wk_s[:, cols],
                    rhs=z_w[:, lo:hi].bitcast(FP8X4), rhs_scale=z_s[:, lo:hi], start=True, stop=True,
                )
            for t in range(SPLIT_TILES):
                if lo == 0:
                    nc.scalar.activation(h_sb[:, t, lo:hi], h_ps[t][:, lo:hi], ACT.Copy, scale=0.0625)
                else:
                    nc.vector.tensor_scalar(h_sb[:, t, lo:hi], h_ps[t][:, lo:hi], 0.0625, None, ALU.mult)
            scatter(n3_l, 1.0, range(SPLIT_TILES), lo, hi)
        for t in range(SPLIT_TILES, PACK):
            nc.vector.tensor_scalar(h_sb[:, t, :], h_ps[t][:], 0.0625, None, ALU.mult)

        pg_n5 = sb([P, PACK, U], F32, "pg_n5")
        y = sb([P, PACK, U], F32, "y")
        y_i = sb([P, U, PACK], BF16, "y_i")
        y_w = sb([P, U], U32, "y_w")
        y_s = sb([P, U], U8, "y_s")
        out_rows = out_0.rearrange("(p t) w -> p t w", t=PACK)
        out_words = out_1[0].rearrange("p c r -> p (c r)").bitcast(I32)

        def subtract(tiles, lo, hi):
            for t in tiles:
                nc.scalar.activation(pg_n5[:, t, lo:hi], pg[t][:].indirect(entries(n5_l, lo, hi)), ACT.Copy)
                nc.vector.tensor_tensor(y[:, t, lo:hi], pg[t][:, lo:hi], pg_n5[:, t, lo:hi], ALU.subtract)

        def store(tiles, lo, hi):
            nc.sync.dma_start(out_rows[:, tiles.start : tiles.stop, lo:hi], y[:, tiles.start : tiles.stop, lo:hi])

        def round_pair(tiles, lo, hi):
            nc.vector.tensor_copy(
                y_i[:, lo:hi, tiles.start : tiles.stop].rearrange("p (c i) t -> p c t i", i=4),
                y[:, tiles.start : tiles.stop, lo:hi].rearrange("p t (c i) -> p c t i", i=4),
            )

        early, late = range(EARLY_TILES), range(EARLY_TILES, PACK)
        scatter(n4_l, 0.5, early, 0, S)
        scatter(n3_l, 1.0, late, 0, S)
        subtract(early, 0, U)
        store(early, 0, U)
        round_pair(early, 0, U)
        scatter(n4_l, 0.5, late, 0, S)
        for lo in range(0, U, PIECE):
            hi = lo + PIECE
            subtract(late, lo, hi)
            if hi % (2 * PIECE) == 0:
                store(late, hi - 2 * PIECE, hi)
            round_pair(late, lo, hi)
            nc.vector.quantize_mx(
                out=y_w[:, lo:hi].bitcast(FP8X4), scales=y_s[:, lo:hi],
                in_=y_i[:, lo:hi, :].rearrange("p c t -> p (c t)"),
            )
            if hi % (2 * PIECE) == 0:
                nc.sync.dma_start(out_words[:, hi - 2 * PIECE : hi], y_w[:, hi - 2 * PIECE : hi].bitcast(I32))
        scale_rows = out_2[0].bitcast(I32)
        for q in range(4):
            eng = nc.sync if q % 2 else nc.scalar
            eng.dma_start(scale_rows[4 * q : 4 * q + 4, :], y_s[:].bitcast(I32)[32 * q : 32 * q + 4, :])
